import numpy as np, ml_dtypes
CORES = [2,10,50,58,66,74,122]
N = 7
VB, TK = 1, 512
def setup_inputs(rng):
    h = (rng.standard_normal((128, TK), dtype=np.float32) / 8).astype(ml_dtypes.bfloat16)
    return {"h": np.broadcast_to(h, (N, 128, TK)).copy(), "w": rng.standard_normal((N, 128, VB * 128), dtype=np.float32).astype(ml_dtypes.bfloat16)}
def reference(h, w):
    H, W = h.astype(np.float64), w.astype(np.float64)
    Z = np.concatenate([W[r].T @ H[r] for r in range(N)], axis=0)
    m = Z.max(axis=0)
    s = np.maximum(Z - 0.5 * m, 0.0).sum(axis=0)
    return {"m": np.broadcast_to(m.astype(np.float32), (N, 1, TK)), "s": np.broadcast_to(s.astype(np.float32), (N, 1, TK))}

@@ -1,0 +1,184 @@
+from concourse.bass import DstId, RemoteDMATransfer
+from concourse.mybir import AluOpType
+
+F32 = "float32"
+SCRATCH = {
+    "hs": ("sbuf", [128, 512], "bfloat16"),
+    "ws": ("sbuf", [128, 128], "bfloat16"),
+    "zp": ("psum", [128, 512], F32),
+    "qa": ("psum", [128, 512], F32),
+    "qb": ("psum", [128, 512], F32),
+    "sa": ("sbuf", [128, 512], F32),
+    "sb": ("sbuf", [128, 512], F32),
+    "land1": ("sbuf", [128, 32], F32),
+    "land2": ("sbuf", [128, 32], F32),
+    "cm": ("sbuf", [128, 32], F32),
+    "cn": ("sbuf", [128, 64], F32),
+    "m4": ("sbuf", [128, 4], F32),
+    "s4": ("sbuf", [128, 4], F32),
+    "cb": ("sbuf", [128, 128], F32),
+    "cs": ("sbuf", [128, 32], F32),
+    "khalf": ("sbuf", [128, 4], F32),
+    "k64": ("sbuf", [128, 4], F32),
+}
+SEMAPHORES = ["ldw", "ldh", "pe", "v", "rdy1", "rdy2", "arr1", "arr2", "loc", "msem", "ssem", "stm", "sts"]
+
+
+def rank_program(g, core, T, topo):
+    rank = T.rank_of(core)
+    if rank is None:
+        return
+    S = T.sem
+    V = g.vector
+    n = len(T.cores)
+    MAX, ADD, SUB, MUL = AluOpType.max, AluOpType.add, AluOpType.subtract, AluOpType.mult
+
+    def hops(dst):
+        a, b = topo.chip(core), topo.chip(dst)
+        return 1 if (topo.mates(a, b) or topo.same_plane(a, b)) else 2
+
+    others = [T.cores[(rank + k) % n] for k in range(1, n)]
+    others.sort(key=lambda d: -hops(d))
+    mask = topo.mask(core, others[0])
+    for d in others:
+        assert topo.may_write(core, d)
+        mask &= topo.mask(core, d)
+    eng = bin(mask).count("1")
+    ids = []
+    for d in others:
+        rid, pid, _se = topo.addr(d)
+        ids.append(DstId(rid=rid, pnc=pid))
+    own = slice(4 * rank, 4 * rank + 4)
+
+    def send(buf, sem):
+        g.remote_dma_fused([RemoteDMATransfer(dst_ids=ids, dma_engine_mask=mask, remote_sem=sem,
+                                              srcs=[buf[:, own]], dsts=[buf[:, own] for _ in others], alu_op=0)],
+                           local_sem=S.loc)
+
+    g.sync.dma_start(T.ws[:], T.w[:]).then_inc(S.ldw, 16)
+    g.scalar.dma_start(T.hs[:], T.h[:]).then_inc(S.ldh, 16)
+
+    g.tensor.wait_ge(S.ldw, 16)
+    g.tensor.wait_ge(S.ldh, 16)
+    for b in range(4):
+        g.tensor.matmul(T.zp[:, b::4], T.hs[:, b::4], T.ws[:], True, True).then_inc(S.pe, 1)
+
+    cnt = [0]
+
+    def sync_v():
+        V.wait_ge(S.v, cnt[0])
+
+    def tt(out, a, b, op, sem=None):
+        i = V.tensor_tensor(out, a, b, op)
+        if sem is None:
+            i.then_inc(S.v, 1)
+            cnt[0] += 1
+        else:
+            i.then_inc(sem, 1)
+
+    def cp(out, a):
+        V.tensor_copy(out, a).then_inc(S.v, 1)
+        cnt[0] += 1
+
+    def fill(ap, val):
+        V.memset(ap, val).then_inc(S.v, 1)
+        cnt[0] += 1
+
+    fill(T.khalf[:], 0.5)
+    fill(T.k64[:], 64.0)
+    fill(T.land2[:, 28:32], 0.0)
+    fill(T.cs[:, 28:32], 0.0)
+
+    zp, qa, qb, sa, sb = T.zp, T.qa, T.qb, T.sa, T.sb
+    V.wait_ge(S.pe, 4)
+    cp(sa[:, 0:256], zp[:, 256:512])
+    sync_v()
+    tt(qa[:, 0:128], zp[:, 0:128], sa[:, 0:128], MAX)
+    tt(sa[:, 256:384], zp[:, 128:256], sa[:, 128:256], MAX)
+    sync_v()
+    tt(qa[:, 128:192], qa[:, 0:64], sa[:, 256:320], MAX)
+    tt(sa[:, 384:448], qa[:, 64:128], sa[:, 320:384], MAX)
+    sync_v()
+    tt(sa[:, 448:512], qa[:, 128:192], sa[:, 384:448], MAX)
+    sync_v()
+    tt(sa[:, 0:32], sa[:, 448:480], sa[:, 480:512], MAX)
+    sync_v()
+    tt(sa[:, 32:48], sa[:, 0:16], sa[:, 16:32], MAX)
+    sync_v()
+    tt(sa[:, 48:56], sa[:, 32:40], sa[:, 40:48], MAX)
+    sync_v()
+    tt(T.land1[:, own], sa[:, 48:52], sa[:, 52:56], MAX, sem=S.rdy1)
+
+    V.wait_ge(S.rdy1, 1)
+    cp(T.land1[:, 28:32], T.land1[:, own])
+    sync_v()
+    V.wait_ge(S.arr1, eng * (n - 1))
+    cm = T.cm
+    tt(cm[:, 0:16], T.land1[:, 0:16], T.land1[:, 16:32], MAX)
+    sync_v()
+    tt(cm[:, 16:24], cm[:, 0:8], cm[:, 8:16], MAX)
+    sync_v()
+    tt(T.m4[:], cm[:, 16:20], cm[:, 20:24], MAX, sem=S.msem)
+    V.wait_ge(S.msem, 1)
+    cb = T.cb
+    tt(cb[:, 0:4], T.m4[:], T.khalf[:], MUL)
+    tt(cb[:, 4:8], T.m4[:], T.khalf[:], MUL)
+    wdt = 8
+    while wdt < 128:
+        sync_v()
+        cp(cb[:, wdt:2 * wdt], cb[:, 0:wdt])
+        wdt *= 2
+    sync_v()
+    tt(qb[:, 0:128], zp[:, 0:128], cb[:], MAX)
+    tt(qb[:, 128:256], zp[:, 128:256], cb[:], MAX)
+    tt(sb[:, 0:128], zp[:, 256:384], cb[:], MAX)
+    tt(sb[:, 128:256], zp[:, 384:512], cb[:], MAX)
+    sync_v()
+    tt(qb[:, 256:384], qb[:, 0:128], sb[:, 0:128], ADD)
+    tt(sb[:, 256:384], qb[:, 128:256], sb[:, 128:256], ADD)
+    sync_v()
+    tt(qb[:, 384:448], qb[:, 256:320], sb[:, 256:320], ADD)
+    tt(sb[:, 384:448], qb[:, 320:384], sb[:, 320:384], ADD)
+    sync_v()
+    tt(sb[:, 448:512], qb[:, 384:448], sb[:, 384:448], ADD)
+    sync_v()
+    tt(sb[:, 0:32], sb[:, 448:480], sb[:, 480:512], ADD)
+    sync_v()
+    tt(sb[:, 32:48], sb[:, 0:16], sb[:, 16:32], ADD)
+    sync_v()
+    tt(sb[:, 48:56], sb[:, 32:40], sb[:, 40:48], ADD)
+    sync_v()
+    tt(T.land2[:, own], sb[:, 48:52], sb[:, 52:56], ADD, sem=S.rdy2)
+
+    cs = T.cs
+    tt(cs[:, 0:4], T.m4[:], T.k64[:], MUL)
+    tt(cs[:, 4:8], T.m4[:], T.k64[:], MUL)
+    sync_v()
+    cp(cs[:, 8:16], cs[:, 0:8])
+    sync_v()
+    cp(cs[:, 16:28], cs[:, 0:12])
+    sync_v()
+
+    V.wait_ge(S.rdy2, 1)
+    V.wait_ge(S.arr2, eng * (n - 1))
+    cn = T.cn
+    tt(cn[:, 0:32], T.land2[:], cs[:], SUB)
+    sync_v()
+    tt(cn[:, 32:48], cn[:, 0:16], cn[:, 16:32], ADD)
+    sync_v()
+    tt(cn[:, 48:56], cn[:, 32:40], cn[:, 40:48], ADD)
+    sync_v()
+    tt(T.s4[:], cn[:, 48:52], cn[:, 52:56], ADD, sem=S.ssem)
+
+    g.wait_ge(S.rdy1, 1)
+    send(T.land1, S.arr1)
+    g.wait_ge(S.rdy2, 1)
+    send(T.land2, S.arr2)
+    g.wait_ge(S.loc, 2 * eng)
+
+    g.scalar.wait_ge(S.msem, 1)
+    g.scalar.dma_start(T.m[:], T.m4[:]).then_inc(S.stm, 16)
+    g.scalar.wait_ge(S.stm, 16)
+    g.sync.wait_ge(S.ssem, 1)
+    g.sync.dma_start(T.s[:], T.s4[:]).then_inc(S.sts, 16)
+    g.sync.wait_ge(S.sts, 16)

@@ -5,23 +5,24 @@ F32 = "float32"
 SCRATCH = {
     "hs": ("sbuf", [128, 512], "bfloat16"),
     "ws": ("sbuf", [128, 128], "bfloat16"),
-    "zp": ("psum", [128, 512], F32),
+    "za": ("psum", [128, 512], F32),
+    "zb": ("psum", [128, 512], F32),
     "qa": ("psum", [128, 512], F32),
     "qb": ("psum", [128, 512], F32),
     "sa": ("sbuf", [128, 512], F32),
     "sb": ("sbuf", [128, 512], F32),
     "land1": ("sbuf", [128, 32], F32),
     "land2": ("sbuf", [128, 32], F32),
-    "cm": ("sbuf", [128, 32], F32),
-    "cn": ("sbuf", [128, 64], F32),
-    "m4": ("sbuf", [128, 4], F32),
+    "y1": ("sbuf", [128, 48], F32),
+    "y2": ("sbuf", [128, 40], F32),
+    "mr": ("sbuf", [128, 36], F32),
+    "cn": ("sbuf", [128, 32], F32),
     "s4": ("sbuf", [128, 4], F32),
     "cb": ("sbuf", [128, 128], F32),
-    "cs": ("sbuf", [128, 32], F32),
-    "khalf": ("sbuf", [128, 4], F32),
-    "k64": ("sbuf", [128, 4], F32),
+    "khalf": ("sbuf", [128, 32], F32),
+    "kneg": ("sbuf", [128, 4], F32),
 }
-SEMAPHORES = ["ldw", "ldh", "pe", "v", "rdy1", "rdy2", "arr1", "arr2", "loc", "msem", "ssem", "stm", "sts"]
+SEMAPHORES = ["ldw", "ldh", "pea", "peb", "v", "rdy1", "rdy2", "arr1", "arr2", "loc", "msem", "ssem", "stm", "sts"]
 
 
 def rank_program(g, core, T, topo):
@@ -31,7 +32,7 @@ def rank_program(g, core, T, topo):
     S = T.sem
     V = g.vector
     n = len(T.cores)
-    MAX, ADD, SUB, MUL = AluOpType.max, AluOpType.add, AluOpType.subtract, AluOpType.mult
+    MAX, ADD, MUL = AluOpType.max, AluOpType.add, AluOpType.mult
 
     def hops(dst):
         a, b = topo.chip(core), topo.chip(dst)
@@ -61,7 +62,9 @@ def rank_program(g, core, T, topo):
     g.tensor.wait_ge(S.ldw, 16)
     g.tensor.wait_ge(S.ldh, 16)
     for b in range(4):
-        g.tensor.matmul(T.zp[:, b::4], T.hs[:, b::4], T.ws[:], True, True).then_inc(S.pe, 1)
+        g.tensor.matmul(T.zb[:, b:256:4], T.hs[:, b::4], T.ws[:, 64:128], True, True).then_inc(S.peb, 1)
+    for b in range(4):
+        g.tensor.matmul(T.za[:, b:256:4], T.hs[:, b::4], T.ws[:, 0:64], True, True).then_inc(S.pea, 1)
 
     cnt = [0]
 
@@ -85,16 +88,15 @@ def rank_program(g, core, T, topo):
         cnt[0] += 1
 
     fill(T.khalf[:], 0.5)
-    fill(T.k64[:], 64.0)
-    fill(T.land2[:, 28:32], 0.0)
-    fill(T.cs[:, 28:32], 0.0)
+    fill(T.kneg[:], -64.0 * n)
 
-    zp, qa, qb, sa, sb = T.zp, T.qa, T.qb, T.sa, T.sb
-    V.wait_ge(S.pe, 4)
-    cp(sa[:, 0:256], zp[:, 256:512])
+    za, zb, qa, qb, sa, sb = T.za, T.zb, T.qa, T.qb, T.sa, T.sb
+    V.wait_ge(S.peb, 4)
+    cp(sa[:, 0:256], zb[:, 0:256])
+    V.wait_ge(S.pea, 4)
     sync_v()
-    tt(qa[:, 0:128], zp[:, 0:128], sa[:, 0:128], MAX)
-    tt(sa[:, 256:384], zp[:, 128:256], sa[:, 128:256], MAX)
+    tt(qa[:, 0:128], za[:, 0:128], sa[:, 0:128], MAX)
+    tt(sa[:, 256:384], za[:, 128:256], sa[:, 128:256], MAX)
     sync_v()
     tt(qa[:, 128:192], qa[:, 0:64], sa[:, 256:320], MAX)
     tt(sa[:, 384:448], qa[:, 64:128], sa[:, 320:384], MAX)
@@ -113,26 +115,22 @@ def rank_program(g, core, T, topo):
     cp(T.land1[:, 28:32], T.land1[:, own])
     sync_v()
     V.wait_ge(S.arr1, eng * (n - 1))
-    cm = T.cm
-    tt(cm[:, 0:16], T.land1[:, 0:16], T.land1[:, 16:32], MAX)
+    y1, y2, mr = T.y1, T.y2, T.mr
+    for k in range(3):
+        tt(y1[:, 16 * k:16 * k + 16], T.land1[:, 0:16], T.land1[:, 16:32], MAX)
     sync_v()
-    tt(cm[:, 16:24], cm[:, 0:8], cm[:, 8:16], MAX)
+    tt(y2[:, 0:40], y1[:, 0:40], y1[:, 8:48], MAX)
     sync_v()
-    tt(T.m4[:], cm[:, 16:20], cm[:, 20:24], MAX, sem=S.msem)
+    tt(mr[:, 0:36], y2[:, 0:36], y2[:, 4:40], MAX, sem=S.msem)
     V.wait_ge(S.msem, 1)
     cb = T.cb
-    tt(cb[:, 0:4], T.m4[:], T.khalf[:], MUL)
-    tt(cb[:, 4:8], T.m4[:], T.khalf[:], MUL)
-    wdt = 8
-    while wdt < 128:
-        sync_v()
-        cp(cb[:, wdt:2 * wdt], cb[:, 0:wdt])
-        wdt *= 2
+    for k in range(4):
+        tt(cb[:, 32 * k:32 * k + 32], mr[:, 0:32], T.khalf[:], MUL)
     sync_v()
-    tt(qb[:, 0:128], zp[:, 0:128], cb[:], MAX)
-    tt(qb[:, 128:256], zp[:, 128:256], cb[:], MAX)
-    tt(sb[:, 0:128], zp[:, 256:384], cb[:], MAX)
-    tt(sb[:, 128:256], zp[:, 384:512], cb[:], MAX)
+    tt(qb[:, 0:128], za[:, 0:128], cb[:], MAX)
+    tt(qb[:, 128:256], za[:, 128:256], cb[:], MAX)
+    tt(sb[:, 0:128], zb[:, 0:128], cb[:], MAX)
+    tt(sb[:, 128:256], zb[:, 128:256], cb[:], MAX)
     sync_v()
     tt(qb[:, 256:384], qb[:, 0:128], sb[:, 0:128], ADD)
     tt(sb[:, 256:384], qb[:, 128:256], sb[:, 128:256], ADD)
@@ -150,25 +148,17 @@ def rank_program(g, core, T, topo):
     sync_v()
     tt(T.land2[:, own], sb[:, 48:52], sb[:, 52:56], ADD, sem=S.rdy2)
 
-    cs = T.cs
-    tt(cs[:, 0:4], T.m4[:], T.k64[:], MUL)
-    tt(cs[:, 4:8], T.m4[:], T.k64[:], MUL)
-    sync_v()
-    cp(cs[:, 8:16], cs[:, 0:8])
-    sync_v()
-    cp(cs[:, 16:28], cs[:, 0:12])
+    tt(T.land2[:, 28:32], mr[:, 0:4], T.kneg[:], MUL)
     sync_v()
 
     V.wait_ge(S.rdy2, 1)
     V.wait_ge(S.arr2, eng * (n - 1))
     cn = T.cn
-    tt(cn[:, 0:32], T.land2[:], cs[:], SUB)
+    tt(cn[:, 0:16], T.land2[:, 0:16], T.land2[:, 16:32], ADD)
     sync_v()
-    tt(cn[:, 32:48], cn[:, 0:16], cn[:, 16:32], ADD)
+    tt(cn[:, 16:24], cn[:, 0:8], cn[:, 8:16], ADD)
     sync_v()
-    tt(cn[:, 48:56], cn[:, 32:40], cn[:, 40:48], ADD)
-    sync_v()
-    tt(T.s4[:], cn[:, 48:52], cn[:, 52:56], ADD, sem=S.ssem)
+    tt(T.s4[:], cn[:, 16:20], cn[:, 20:24], ADD, sem=S.ssem)
 
     g.wait_ge(S.rdy1, 1)
     send(T.land1, S.arr1)
@@ -177,7 +167,7 @@ def rank_program(g, core, T, topo):
     g.wait_ge(S.loc, 2 * eng)
 
     g.scalar.wait_ge(S.msem, 1)
-    g.scalar.dma_start(T.m[:], T.m4[:]).then_inc(S.stm, 16)
+    g.scalar.dma_start(T.m[:], mr[:, 0:4]).then_inc(S.stm, 16)
     g.scalar.wait_ge(S.stm, 16)
     g.sync.wait_ge(S.ssem, 1)
     g.sync.dma_start(T.s[:], T.s4[:]).then_inc(S.sts, 16)

from concourse.bass import DstId, RemoteDMATransfer
from concourse.mybir import AluOpType

F32 = "float32"
SCRATCH = {
    "hs": ("sbuf", [128, 512], "bfloat16"),
    "ws": ("sbuf", [128, 128], "bfloat16"),
    "za": ("psum", [128, 512], F32),
    "zb": ("psum", [128, 512], F32),
    "qa": ("psum", [128, 512], F32),
    "qb": ("psum", [128, 512], F32),
    "sa": ("sbuf", [128, 512], F32),
    "sb": ("sbuf", [128, 512], F32),
    "land1": ("sbuf", [128, 32], F32),
    "land2": ("sbuf", [128, 32], F32),
    "y1": ("sbuf", [128, 48], F32),
    "y2": ("sbuf", [128, 40], F32),
    "mr": ("sbuf", [128, 36], F32),
    "cn": ("sbuf", [128, 32], F32),
    "s4": ("sbuf", [128, 4], F32),
    "cb": ("sbuf", [128, 128], F32),
    "khalf": ("sbuf", [128, 32], F32),
    "kneg": ("sbuf", [128, 4], F32),
}
SEMAPHORES = ["ldw", "ldh", "pea", "peb", "v", "rdy1", "rdy2", "arr1", "arr2", "loc", "msem", "ssem", "stm", "sts"]


def rank_program(g, core, T, topo):
    rank = T.rank_of(core)
    if rank is None:
        return
    S = T.sem
    V = g.vector
    n = len(T.cores)
    MAX, ADD, MUL = AluOpType.max, AluOpType.add, AluOpType.mult

    def hops(dst):
        a, b = topo.chip(core), topo.chip(dst)
        return 1 if (topo.mates(a, b) or topo.same_plane(a, b)) else 2

    others = [T.cores[(rank + k) % n] for k in range(1, n)]
    others.sort(key=lambda d: -hops(d))
    mask = topo.mask(core, others[0])
    for d in others:
        assert topo.may_write(core, d)
        mask &= topo.mask(core, d)
    eng = bin(mask).count("1")
    ids = []
    for d in others:
        rid, pid, _se = topo.addr(d)
        ids.append(DstId(rid=rid, pnc=pid))
    own = slice(4 * rank, 4 * rank + 4)

    def send(buf, sem):
        g.remote_dma_fused([RemoteDMATransfer(dst_ids=ids, dma_engine_mask=mask, remote_sem=sem,
                                              srcs=[buf[:, own]], dsts=[buf[:, own] for _ in others], alu_op=0)],
                           local_sem=S.loc)

    g.sync.dma_start(T.ws[:], T.w[:]).then_inc(S.ldw, 16)
    g.scalar.dma_start(T.hs[:], T.h[:]).then_inc(S.ldh, 16)

    g.tensor.wait_ge(S.ldw, 16)
    g.tensor.wait_ge(S.ldh, 16)
    for b in range(4):
        g.tensor.matmul(T.zb[:, b:256:4], T.hs[:, b::4], T.ws[:, 64:128], True, True).then_inc(S.peb, 1)
    for b in range(4):
        g.tensor.matmul(T.za[:, b:256:4], T.hs[:, b::4], T.ws[:, 0:64], True, True).then_inc(S.pea, 1)

    cnt = [0]

    def sync_v():
        V.wait_ge(S.v, cnt[0])

    def tt(out, a, b, op, sem=None):
        i = V.tensor_tensor(out, a, b, op)
        if sem is None:
            i.then_inc(S.v, 1)
            cnt[0] += 1
        else:
            i.then_inc(sem, 1)

    def cp(out, a):
        V.tensor_copy(out, a).then_inc(S.v, 1)
        cnt[0] += 1

    def fill(ap, val):
        V.memset(ap, val).then_inc(S.v, 1)
        cnt[0] += 1

    fill(T.khalf[:], 0.5)
    fill(T.kneg[:], -64.0 * n)

    za, zb, qa, qb, sa, sb = T.za, T.zb, T.qa, T.qb, T.sa, T.sb
    V.wait_ge(S.peb, 4)
    cp(sa[:, 0:256], zb[:, 0:256])
    V.wait_ge(S.pea, 4)
    sync_v()
    tt(qa[:, 0:128], za[:, 0:128], sa[:, 0:128], MAX)
    tt(sa[:, 256:384], za[:, 128:256], sa[:, 128:256], MAX)
    sync_v()
    tt(qa[:, 128:192], qa[:, 0:64], sa[:, 256:320], MAX)
    tt(sa[:, 384:448], qa[:, 64:128], sa[:, 320:384], MAX)
    sync_v()
    tt(sa[:, 448:512], qa[:, 128:192], sa[:, 384:448], MAX)
    sync_v()
    tt(sa[:, 0:32], sa[:, 448:480], sa[:, 480:512], MAX)
    sync_v()
    tt(sa[:, 32:48], sa[:, 0:16], sa[:, 16:32], MAX)
    sync_v()
    tt(sa[:, 48:56], sa[:, 32:40], sa[:, 40:48], MAX)
    sync_v()
    tt(T.land1[:, own], sa[:, 48:52], sa[:, 52:56], MAX, sem=S.rdy1)

    V.wait_ge(S.rdy1, 1)
    cp(T.land1[:, 28:32], T.land1[:, own])
    sync_v()
    V.wait_ge(S.arr1, eng * (n - 1))
    y1, y2, mr = T.y1, T.y2, T.mr
    for k in range(3):
        tt(y1[:, 16 * k:16 * k + 16], T.land1[:, 0:16], T.land1[:, 16:32], MAX)
    sync_v()
    tt(y2[:, 0:40], y1[:, 0:40], y1[:, 8:48], MAX)
    sync_v()
    tt(mr[:, 0:36], y2[:, 0:36], y2[:, 4:40], MAX, sem=S.msem)
    V.wait_ge(S.msem, 1)
    cb = T.cb
    for k in range(4):
        tt(cb[:, 32 * k:32 * k + 32], mr[:, 0:32], T.khalf[:], MUL)
    sync_v()
    tt(qb[:, 0:128], za[:, 0:128], cb[:], MAX)
    tt(qb[:, 128:256], za[:, 128:256], cb[:], MAX)
    tt(sb[:, 0:128], zb[:, 0:128], cb[:], MAX)
    tt(sb[:, 128:256], zb[:, 128:256], cb[:], MAX)
    sync_v()
    tt(qb[:, 256:384], qb[:, 0:128], sb[:, 0:128], ADD)
    tt(sb[:, 256:384], qb[:, 128:256], sb[:, 128:256], ADD)
    sync_v()
    tt(qb[:, 384:448], qb[:, 256:320], sb[:, 256:320], ADD)
    tt(sb[:, 384:448], qb[:, 320:384], sb[:, 320:384], ADD)
    sync_v()
    tt(sb[:, 448:512], qb[:, 384:448], sb[:, 384:448], ADD)
    sync_v()
    tt(sb[:, 0:32], sb[:, 448:480], sb[:, 480:512], ADD)
    sync_v()
    tt(sb[:, 32:48], sb[:, 0:16], sb[:, 16:32], ADD)
    sync_v()
    tt(sb[:, 48:56], sb[:, 32:40], sb[:, 40:48], ADD)
    sync_v()
    tt(T.land2[:, own], sb[:, 48:52], sb[:, 52:56], ADD, sem=S.rdy2)

    tt(T.land2[:, 28:32], mr[:, 0:4], T.kneg[:], MUL)
    sync_v()

    V.wait_ge(S.rdy2, 1)
    V.wait_ge(S.arr2, eng * (n - 1))
    cn = T.cn
    tt(cn[:, 0:16], T.land2[:, 0:16], T.land2[:, 16:32], ADD)
    sync_v()
    tt(cn[:, 16:24], cn[:, 0:8], cn[:, 8:16], ADD)
    sync_v()
    tt(T.s4[:], cn[:, 16:20], cn[:, 20:24], ADD, sem=S.ssem)

    g.wait_ge(S.rdy1, 1)
    send(T.land1, S.arr1)
    g.wait_ge(S.rdy2, 1)
    send(T.land2, S.arr2)
    g.wait_ge(S.loc, 2 * eng)

    g.scalar.wait_ge(S.msem, 1)
    g.scalar.dma_start(T.m[:], mr[:, 0:4]).then_inc(S.stm, 16)
    g.scalar.wait_ge(S.stm, 16)
    g.sync.wait_ge(S.ssem, 1)
    g.sync.dma_start(T.s[:], T.s4[:]).then_inc(S.sts, 16)
    g.sync.wait_ge(S.sts, 16)
